import numpy as np
import ml_dtypes


def mxq(x, axis, fmt="e4m3"):
    dtype, down = {"e4m3": (ml_dtypes.float8_e4m3fn, 7), "e5m2": (ml_dtypes.float8_e5m2, 14)}[fmt]
    v = np.moveaxis(np.asarray(x, np.float32).astype(ml_dtypes.bfloat16).astype(np.float64), axis, -1)
    blocks = v.reshape(v.shape[:-1] + (-1, 32))
    amax = np.abs(blocks).max(-1, keepdims=True)
    byte = np.maximum(np.where(amax > 0, np.frexp(amax)[1] - 1 + 127, 0) - down, 1)
    scale = np.exp2(byte - 127.0)
    codes = (blocks / scale).astype(np.float32).astype(dtype).astype(np.float64)
    return np.moveaxis((codes * scale).reshape(v.shape), -1, axis)


WIDE = False


def mx_kscale(k):
    if not WIDE:
        return np.ones(k)
    levels = np.array([10, -10, 5, -5, 0])
    if k % 512:
        return np.exp2(np.random.permutation(np.resize(levels, k // 32))).repeat(32)
    a = np.empty((k // 512, 16))
    for p in range(k // 512):
        a[p, :8] = np.random.permutation(np.resize(levels, 8))
        for g in range(8):
            far = levels[np.abs(levels - a[p, g]) >= 10]
            a[p, g + 8] = far[np.random.randint(len(far))]
    return np.exp2(a.ravel()).repeat(32)


def f64(x):
    return np.asarray(x).astype(np.float64)


def striped(idx):
    return np.tile(np.asarray(idx).reshape(-1, 16).T, (8, 1)).astype(np.uint16)


def unstriped(offs):
    return offs[:16].T.reshape(-1).astype(np.int64)


def striped8(idx):
    return np.asarray(idx).reshape(8, -1, 16).transpose(0, 2, 1).reshape(128, -1).astype(np.uint16)


def unstriped8(offs):
    return offs.reshape(8, 16, -1).transpose(0, 2, 1).reshape(8, -1).astype(np.int64)


def pick8(x, idx, run):
    r = np.arange(len(x))
    return x[r[:, None], idx[r % (8 * run) // run]]


E2M1 = np.array([0.0, 0.5, 1.0, 1.5, 2.0, 3.0, 4.0, 6.0, -0.0, -0.5, -1.0, -1.5, -2.0, -3.0, -4.0, -6.0])


def pack_weight(w, fmt):
    k, n = w.shape
    w = f64(np.asarray(w, np.float32).astype(ml_dtypes.bfloat16)).reshape(k // 32, 32, n)
    amax = np.abs(w).max(1)
    if fmt == "e4m3":
        byte = np.frexp(amax)[1] - 1 + 127 - 7
    else:
        mant, ex = np.frexp(amax / 6.0)
        byte = np.where(mant > 0.5, ex, ex - 1) + 127
    byte = np.clip(np.where(amax > 0, byte, 1), 1, 254)
    scaled = (w * np.exp2(127.0 - byte)[:, None, :]).reshape(k, n).astype(np.float32)
    by_word = np.ascontiguousarray(scaled.reshape(k // 512, 128, 4, n).transpose(0, 1, 3, 2))
    if fmt == "e4m3":
        words = by_word.astype(ml_dtypes.float8_e4m3fn).view(np.uint8)
    else:
        c = by_word.astype(ml_dtypes.float4_e2m1fn).view(np.uint8) & 0xF
        words = (c[..., 0::2] | (c[..., 1::2] << 4)).reshape(k // 512, 128, 2 * n)
    return np.ascontiguousarray(words), np.ascontiguousarray(byte.astype(np.uint8).reshape(k // 512, 16, n))


def unpack_weight(words, scales, fmt):
    g, _, n = scales.shape
    words = np.ascontiguousarray(words).reshape(g, 128, n, -1)
    if fmt == "e4m3":
        vals = words.view(ml_dtypes.float8_e4m3fn).astype(np.float64)
    else:
        nib = np.empty((g, 128, n, 4), np.uint8)
        nib[..., 0::2] = words & 0xF
        nib[..., 1::2] = words >> 4
        vals = E2M1[nib]
    vals = vals * np.repeat(np.exp2(scales.astype(np.float64) - 127.0), 8, axis=1)[..., None]
    return vals.transpose(0, 1, 3, 2).reshape(g * 512, n)


def sgn(shape):
    return np.random.uniform(0.5, 2.0, shape) * np.where(np.random.standard_normal(shape) < 0, -1.0, 1.0)


K, J, R, T, U, Z, M, O, N, E, G = 512, 512, 512, 1024, 1024, 512, 1024, 256, 256, 128, 512


def setup_inputs():
    n = np.random.standard_normal
    idx = np.stack([np.random.permutation(T)[:J] for _ in range(8)])
    idx2 = np.stack([np.random.permutation(U)[:J] for _ in range(8)])
    idx3 = np.random.permutation(M)[:J]
    idx4 = np.stack([np.random.permutation(J)[:O] for _ in range(8)])
    idx5 = np.stack([np.random.permutation(O)[:E] for _ in range(8)])
    idx6 = np.stack([np.random.permutation(G)[:E] for _ in range(8)])
    fk = mx_kscale(K)
    fr = mx_kscale(R)
    fz = mx_kscale(Z)
    wp = pack_weight(n((K, R)) * 1 / np.sqrt(K) / fk[:, None] * fr, "e2m1")
    xop = pack_weight(n((Z, M)) / fz[:, None], "e2m1")
    w2p = pack_weight(n((Z, R)) * 1 / np.sqrt(Z) * fz[:, None] * fr, "e4m3")
    wbp = pack_weight(n((R, N)) * 1 / np.sqrt(R) / fr[:, None], "e4m3")
    return {
        "ta": (np.random.randint(-7, 8, (K, T)).astype(np.float64)).astype(np.float32),
        "tb": (np.random.randint(1, 9, (K, U)).astype(np.float64)).astype(np.float32),
        "ga": ((np.random.randint(8, 25, (K, 1)) / 64.0) * fk[:, None]).astype(np.float32),
        "gb": (np.random.uniform(0.1, 0.4, (K, 1))).astype(np.float32),
        "w_words": wp[0],
        "w_scales": wp[1],
        "xo_words": xop[0],
        "xo_scales": xop[1],
        "w2_words": w2p[0],
        "w2_scales": w2p[1],
        "sa": (np.random.uniform(0.5, 1.6, (R, 1))).astype(np.float32),
        "wb_words": wbp[0],
        "wb_scales": wbp[1],
        "so": (sgn((N, 1))).astype(np.float32),
        "offs": striped8(idx),
        "offs2": striped8(idx2),
        "offs3": striped(idx3),
        "offs4": striped8(idx4),
        "offs5": striped8(idx5),
        "offs6": striped8(idx6),
    }


def reference(ta, tb, ga, gb, w_words, w_scales, xo_words, xo_scales, w2_words, w2_scales, sa, wb_words, wb_scales, so, offs, offs2, offs3, offs4, offs5, offs6):
    idx = unstriped8(offs)
    idx2 = unstriped8(offs2)
    idx3 = unstriped(offs3)
    idx4 = unstriped8(offs4)
    idx5 = unstriped8(offs5)
    idx6 = unstriped8(offs6)
    wu = unpack_weight(w_words, w_scales, "e2m1")
    xou = unpack_weight(xo_words, xo_scales, "e2m1")
    w2u = unpack_weight(w2_words, w2_scales, "e4m3")
    wbu = unpack_weight(wb_words, wb_scales, "e4m3")
    xc = pick8(f64(ta), idx, 64) * f64(ga) * pick8(f64(tb), idx2, 64) * f64(gb)
    xcq = mxq(xc, 0, "e4m3")
    xoidx3g = xou[:, idx3]
    a = wu.T @ xcq + w2u.T @ xoidx3g
    g1 = np.maximum(a, 0.0)
    hid = pick8(g1, idx4, 64) * f64(sa)
    hidq = mxq(hid, 0, "e4m3")
    p = wbu.T @ hidq
    m0 = pick8(p, idx5, 16) * f64(so)
    y = np.zeros((N, G))
    y[np.arange(N)[:, None], idx6[np.arange(N) % 128 // 16]] = m0
    return y

@@ -1,0 +1,190 @@
+from contextlib import ExitStack
+
+import concourse.mybir as mybir
+
+K, J, R, T, M, O, N, E, G = 512, 512, 512, 1024, 1024, 256, 256, 128, 512
+P = 128
+PACK = 4
+HALF = J // 2
+
+F32 = mybir.dt.float32
+BF16 = mybir.dt.bfloat16
+I32 = mybir.dt.int32
+U32 = mybir.dt.uint32
+U16 = mybir.dt.uint16
+U8 = mybir.dt.uint8
+FP8X4 = mybir.dt.float8_e4m3fn_x4
+FP4X4 = mybir.dt.float4_e2m1fn_x4
+ACT = mybir.ActivationFunctionType
+ALU = mybir.AluOpType
+
+FLOPS = 2 * K * R * J * 2 + 2 * R * N * O
+
+
+def tile_picked_codegain_plain_bank_kept_one_posted_kernel(
+    tc, ta, tb, ga, gb, w_words, w_scales, xo_words, xo_scales, w2_words, w2_scales, sa,
+    wb_words, wb_scales, so, offs, offs2, offs3, offs4, offs5, offs6, out,
+):
+    nc = tc.nc
+    with ExitStack() as ctx:
+        sb = ctx.enter_context(tc.tile_pool(name="sb", bufs=1))
+        ps = ctx.enter_context(tc.psum_pool(name="ps", bufs=1))
+
+        def load_list(src, name):
+            t = sb.tile(list(src.shape), U16, name=name)
+            nc.sync.dma_start(t[:], src)
+            return t
+
+        def load_col4(src, name, queue):
+            t = sb.tile([P, PACK], F32, name=name)
+            queue.dma_start(out=t[:], in_=src.rearrange("(p j) o -> p (j o)", j=PACK))
+            return t
+
+        def load_table(src, t, name):
+            tl = sb.tile([P, T], F32, name=name)
+            nc.sync.dma_start(out=tl[:], in_=src.rearrange("(p j) c -> p j c", j=PACK)[:, t, :])
+            return tl
+
+        def zero_plane(width, name):
+            pl = sb.tile([P, width], U8, name=name, align_bytes=64)
+            nc.vector.memset(pl[:].bitcast(I32), 0)
+            return pl
+
+        def load_plane(pl, src):
+            for r in range(4):
+                nc.sync.dma_start(out=pl[r:P:32, :].bitcast(I32), in_=src[0, r:16:4, :].bitcast(I32))
+
+        xs_win = zero_plane(M, "xs_win")
+        w2s_raw = zero_plane(R, "w2s_raw")
+        ws_raw = zero_plane(R, "ws_raw")
+        wbs = zero_plane(N, "wbs")
+        pages = [sb.tile([P, G], F32, name="page%d" % t) for t in range(2)]
+        for pg in pages:
+            nc.vector.memset(pg[:], 0.0)
+
+        tas, tbs = [None] * PACK, [None] * PACK
+        l1 = load_list(offs, "l1")
+        ga_t = load_col4(ga, "ga_t", nc.scalar)
+        tas[0] = load_table(ta, 0, "ta0")
+        l2 = load_list(offs2, "l2")
+        gb_t = load_col4(gb, "gb_t", nc.scalar)
+        tbs[0] = load_table(tb, 0, "tb0")
+        l3 = load_list(offs3, "l3")
+        xw_win = sb.tile([P, M], U16, name="xw_win", align_bytes=64)
+        nc.sync.dma_start(out=xw_win[:].bitcast(I32), in_=xo_words[0].bitcast(I32))
+        load_plane(xs_win, xo_scales)
+        tas[1] = load_table(ta, 1, "ta1")
+        tbs[1] = load_table(tb, 1, "tb1")
+        tas[2] = load_table(ta, 2, "ta2")
+        load_plane(ws_raw, w_scales)
+        tbs[2] = load_table(tb, 2, "tb2")
+        w2_raw = sb.tile([P, R], U32, name="w2_raw", align_bytes=64)
+        nc.sync.dma_start(out=w2_raw[:].bitcast(I32), in_=w2_words[0].rearrange("p c b -> p (c b)").bitcast(I32))
+        load_plane(w2s_raw, w2_scales)
+        tas[3] = load_table(ta, 3, "ta3")
+        tbs[3] = load_table(tb, 3, "tb3")
+        w_raw = sb.tile([P, R], U16, name="w_raw", align_bytes=64)
+        nc.sync.dma_start(out=w_raw[:].bitcast(I32), in_=w_words[0].bitcast(I32))
+        l4 = load_list(offs4, "l4")
+        sa_t = load_col4(sa, "sa_t", nc.sync)
+        wb_t = sb.tile([P, N], U32, name="wb_t", align_bytes=64)
+        nc.sync.dma_start(out=wb_t[:].bitcast(I32), in_=wb_words[0].rearrange("p c b -> p (c b)").bitcast(I32))
+        load_plane(wbs, wb_scales)
+        l5 = load_list(offs5, "l5")
+        l6 = load_list(offs6, "l6")
+        so_t = sb.tile([P, 2], F32, name="so_t")
+        with nc.allow_non_contiguous_dma(reason="one value a partition for each tile of 128 rows"):
+            nc.sync.dma_start(out=so_t[:], in_=so.rearrange("(t p) o -> p (t o)", p=P))
+
+        av = [[sb.tile([P, 2, HALF], F32, name="av%d%d" % (u, h)) for h in range(2)] for u in range(2)]
+        bv = [[sb.tile([P, 2, HALF], F32, name="bv%d%d" % (u, h)) for h in range(2)] for u in range(2)]
+        xc = [sb.tile([P, HALF, PACK], BF16, name="xc%d" % h, align_bytes=64) for h in range(2)]
+        xq = sb.tile([P, J], U32, name="xq", align_bytes=64)
+        xqs = sb.tile([P, J], U8, name="xqs", align_bytes=64)
+
+        def fetch(dst, table, lst, scale, t):
+            for h in range(2):
+                nc.scalar.activation(
+                    out=dst[t // 2][h][:, t % 2, :],
+                    in_=table[:].indirect(lst[:, h * (HALF // 16):(h + 1) * (HALF // 16)]),
+                    func=ACT.Copy, scale=scale[:, t:t + 1])
+
+        def product(u, h):
+            nc.vector.tensor_tensor(
+                out=xc[h][:, :, 2 * u:2 * u + 2],
+                in0=av[u][h][:].rearrange("p t j -> p j t"),
+                in1=bv[u][h][:].rearrange("p t j -> p j t"),
+                op=ALU.mult)
+
+        xw = sb.tile([P, J], U16, name="xw", align_bytes=64)
+        xs = sb.tile([P, J], U8, name="xs", align_bytes=64)
+        nc.vector.tensor_copy(out=xw[:], in_=xw_win[:].indirect(l3[:]))
+        nc.vector.tensor_copy(out=xs[:], in_=xs_win[:].indirect(l3[:]))
+
+        for t in range(2):
+            fetch(av, tas[t], l1, ga_t, t)
+            fetch(bv, tbs[t], l2, gb_t, t)
+        for h in range(2):
+            product(0, h)
+
+        w2_d = sb.tile([P, R], U32, name="w2_d", align_bytes=64)
+        w2s_d = sb.tile([P, R], U8, name="w2s_d", align_bytes=64)
+        w_d = sb.tile([P, R], U16, name="w_d", align_bytes=64)
+        ws_d = sb.tile([P, R], U8, name="ws_d", align_bytes=64)
+        for dst, raw in ((ws_d, ws_raw), (w2_d, w2_raw), (w2s_d, w2s_raw)):
+            nc.vector.tensor_copy(out=dst[:].rearrange("p (t m) -> p t m", t=PACK),
+                                  in_=raw[:].rearrange("p (m t) -> p t m", t=PACK))
+
+        parts = [(0, 0, HALF), (0, HALF, HALF), (1, 0, J), (2, 0, J), (3, 0, J)]
+        acc = [ps.tile([P, wd], F32, name="acc%d" % i) for i, (t, c0, wd) in enumerate(parts)]
+        for i, (t, c0, wd) in enumerate(parts):
+            nc.tensor.matmul_mx(out=acc[i][:], lhsT=w2_d[:, t * P:(t + 1) * P].bitcast(FP8X4),
+                                lhsT_scale=w2s_d[:, t * P:(t + 1) * P],
+                                rhs=xw[:, c0:c0 + wd].bitcast(FP4X4), rhs_scale=xs[:, c0:c0 + wd],
+                                start=True, stop=False)
+
+        for t in range(2, 4):
+            fetch(av, tas[t], l1, ga_t, t)
+            fetch(bv, tbs[t], l2, gb_t, t)
+        nc.scalar.copy(out=w_d[:].rearrange("p (t m) -> p t m", t=PACK), in_=w_raw[:].rearrange("p (m t) -> p t m", t=PACK))
+        for h in range(2):
+            product(1, h)
+        for h in range(2):
+            nc.vector.quantize_mx(out=xq[:, h * HALF:(h + 1) * HALF].bitcast(FP8X4),
+                                  scales=xqs[:, h * HALF:(h + 1) * HALF],
+                                  in_=xc[h][:].rearrange("p j t -> p (j t)"))
+
+        g1 = [sb.tile([P, J], F32, name="g1_%d" % t) for t in range(PACK)]
+        for i, (t, c0, wd) in enumerate(parts):
+            nc.tensor.matmul_mx(out=acc[i][:], lhsT=w_d[:, t * P:(t + 1) * P].bitcast(FP4X4),
+                                lhsT_scale=ws_d[:, t * P:(t + 1) * P],
+                                rhs=xq[:, c0:c0 + wd].bitcast(FP8X4), rhs_scale=xqs[:, c0:c0 + wd],
+                                start=False, stop=True)
+            if i == 0:
+                nc.scalar.activation(out=g1[t][:, c0:c0 + wd], in_=acc[i][:], func=ACT.Relu)
+            else:
+                nc.vector.tensor_scalar(out=g1[t][:, c0:c0 + wd], in0=acc[i][:], scalar1=0.0, scalar2=None, op0=ALU.max)
+
+        hv = [sb.tile([P, 2, O], BF16, name="hv%d" % u) for u in range(2)]
+        hid = sb.tile([P, O, PACK], BF16, name="hid", align_bytes=64)
+        for t in range(PACK):
+            nc.scalar.activation(out=hv[t // 2][:, t % 2, :], in_=g1[t][:].indirect(l4[:]),
+                                 func=ACT.Copy, scale=sa_t[:, t:t + 1])
+            if t % 2 == 1:
+                nc.vector.tensor_copy(out=hid[:, :, t - 1:t + 1], in_=hv[t // 2][:].rearrange("p t j -> p j t"))
+        hq = sb.tile([P, O], U32, name="hq", align_bytes=64)
+        hqs = sb.tile([P, O], U8, name="hqs", align_bytes=64)
+        nc.vector.quantize_mx(out=hq[:].bitcast(FP8X4), scales=hqs[:], in_=hid[:].rearrange("p j t -> p (j t)"))
+
+        pacc = [ps.tile([P, O], F32, name="pacc%d" % t) for t in range(2)]
+        pv = [sb.tile([P, O], F32, name="pv%d" % t) for t in range(2)]
+        m0 = [sb.tile([P, E], F32, name="m0_%d" % t) for t in range(2)]
+        for t in range(2):
+            nc.tensor.matmul_mx(out=pacc[t][:], lhsT=wb_t[:, t * P:(t + 1) * P].bitcast(FP8X4),
+                                lhsT_scale=wbs[:, t * P:(t + 1) * P],
+                                rhs=hq[:].bitcast(FP8X4), rhs_scale=hqs[:], start=True, stop=True)
+            nc.vector.tensor_copy(out=pv[t][:], in_=pacc[t][:])
+            nc.scalar.activation(out=m0[t][:], in_=pv[t][:].indirect(l5[:]), func=ACT.Copy, scale=so_t[:, t:t + 1])
+        for t in range(2):
+            nc.vector.tensor_copy(out=pages[t][:].indirect(l6[:]), in_=m0[t][:])
+            nc.sync.dma_start(out=out[t * P:(t + 1) * P, :], in_=pages[t][:])

@@ -54,41 +54,47 @@ def tile_picked_codegain_plain_bank_kept_one_posted_kernel(
             for r in range(4):
                 nc.sync.dma_start(out=pl[r:P:32, :].bitcast(I32), in_=src[0, r:16:4, :].bitcast(I32))
 
+        def load_words(src, width, dtype, name):
+            tl = sb.tile([P, width], dtype, name=name, align_bytes=64)
+            nc.sync.dma_start(out=tl[:].bitcast(I32), in_=src.bitcast(I32))
+            return tl
+
+        def deal(copy, raw, name, walk="t m"):
+            dst = sb.tile(list(raw.shape), raw.dtype, name=name, align_bytes=64)
+            copy(out=dst[:].rearrange("p (t m) -> p " + walk, t=PACK), in_=raw[:].rearrange("p (m t) -> p " + walk, t=PACK))
+            return dst
+
         xs_win = zero_plane(M, "xs_win")
-        w2s_raw = zero_plane(R, "w2s_raw")
         ws_raw = zero_plane(R, "ws_raw")
+        w2s_raw = zero_plane(R, "w2s_raw")
         wbs = zero_plane(N, "wbs")
         pages = [sb.tile([P, G], F32, name="page%d" % t) for t in range(2)]
         for pg in pages:
             nc.vector.memset(pg[:], 0.0)
 
         tas, tbs = [None] * PACK, [None] * PACK
+        tas[0] = load_table(ta, 0, "ta0")
         l1 = load_list(offs, "l1")
         ga_t = load_col4(ga, "ga_t", nc.scalar)
-        tas[0] = load_table(ta, 0, "ta0")
+        tbs[0] = load_table(tb, 0, "tb0")
         l2 = load_list(offs2, "l2")
         gb_t = load_col4(gb, "gb_t", nc.scalar)
-        tbs[0] = load_table(tb, 0, "tb0")
-        l3 = load_list(offs3, "l3")
-        xw_win = sb.tile([P, M], U16, name="xw_win", align_bytes=64)
-        nc.sync.dma_start(out=xw_win[:].bitcast(I32), in_=xo_words[0].bitcast(I32))
-        load_plane(xs_win, xo_scales)
         tas[1] = load_table(ta, 1, "ta1")
+        xw_win = load_words(xo_words[0], M, U16, "xw_win")
+        l3 = load_list(offs3, "l3")
+        load_plane(xs_win, xo_scales)
         tbs[1] = load_table(tb, 1, "tb1")
         tas[2] = load_table(ta, 2, "ta2")
         load_plane(ws_raw, w_scales)
         tbs[2] = load_table(tb, 2, "tb2")
-        w2_raw = sb.tile([P, R], U32, name="w2_raw", align_bytes=64)
-        nc.sync.dma_start(out=w2_raw[:].bitcast(I32), in_=w2_words[0].rearrange("p c b -> p (c b)").bitcast(I32))
-        load_plane(w2s_raw, w2_scales)
+        w2_raw = load_words(w2_words[0].rearrange("p c b -> p (c b)"), R, U32, "w2_raw")
         tas[3] = load_table(ta, 3, "ta3")
+        load_plane(w2s_raw, w2_scales)
         tbs[3] = load_table(tb, 3, "tb3")
-        w_raw = sb.tile([P, R], U16, name="w_raw", align_bytes=64)
-        nc.sync.dma_start(out=w_raw[:].bitcast(I32), in_=w_words[0].bitcast(I32))
+        w_raw = load_words(w_words[0], R, U16, "w_raw")
         l4 = load_list(offs4, "l4")
         sa_t = load_col4(sa, "sa_t", nc.sync)
-        wb_t = sb.tile([P, N], U32, name="wb_t", align_bytes=64)
-        nc.sync.dma_start(out=wb_t[:].bitcast(I32), in_=wb_words[0].rearrange("p c b -> p (c b)").bitcast(I32))
+        wb_t = load_words(wb_words[0].rearrange("p c b -> p (c b)"), N, U32, "wb_t")
         load_plane(wbs, wb_scales)
         l5 = load_list(offs5, "l5")
         l6 = load_list(offs6, "l6")
@@ -96,24 +102,21 @@ def tile_picked_codegain_plain_bank_kept_one_posted_kernel(
         with nc.allow_non_contiguous_dma(reason="one value a partition for each tile of 128 rows"):
             nc.sync.dma_start(out=so_t[:], in_=so.rearrange("(t p) o -> p (t o)", p=P))
 
-        av = [[sb.tile([P, 2, HALF], F32, name="av%d%d" % (u, h)) for h in range(2)] for u in range(2)]
-        bv = [[sb.tile([P, 2, HALF], F32, name="bv%d%d" % (u, h)) for h in range(2)] for u in range(2)]
+        av = [sb.tile([P, 2, J], F32, name="av%d" % u) for u in range(2)]
+        bv0 = sb.tile([P, 2, J], F32, name="bv0")
+        bv1 = [sb.tile([P, 2, HALF], F32, name="bv1%d" % h) for h in range(2)]
         xc = [sb.tile([P, HALF, PACK], BF16, name="xc%d" % h, align_bytes=64) for h in range(2)]
         xq = sb.tile([P, J], U32, name="xq", align_bytes=64)
         xqs = sb.tile([P, J], U8, name="xqs", align_bytes=64)
 
-        def fetch(dst, table, lst, scale, t):
-            for h in range(2):
-                nc.scalar.activation(
-                    out=dst[t // 2][h][:, t % 2, :],
-                    in_=table[:].indirect(lst[:, h * (HALF // 16):(h + 1) * (HALF // 16)]),
-                    func=ACT.Copy, scale=scale[:, t:t + 1])
+        def fetch(dst, table, offsets, scale, t):
+            nc.scalar.activation(out=dst, in_=table[:].indirect(offsets), func=ACT.Copy, scale=scale[:, t:t + 1])
 
-        def product(u, h):
+        def product(u, h, b_pair):
             nc.vector.tensor_tensor(
                 out=xc[h][:, :, 2 * u:2 * u + 2],
-                in0=av[u][h][:].rearrange("p t j -> p j t"),
-                in1=bv[u][h][:].rearrange("p t j -> p j t"),
+                in0=av[u][:, :, h * HALF:(h + 1) * HALF].rearrange("p t j -> p j t"),
+                in1=b_pair.rearrange("p t j -> p j t"),
                 op=ALU.mult)
 
         xw = sb.tile([P, J], U16, name="xw", align_bytes=64)
@@ -122,37 +125,35 @@ def tile_picked_codegain_plain_bank_kept_one_posted_kernel(
         nc.vector.tensor_copy(out=xs[:], in_=xs_win[:].indirect(l3[:]))
 
         for t in range(2):
-            fetch(av, tas[t], l1, ga_t, t)
-            fetch(bv, tbs[t], l2, gb_t, t)
+            fetch(av[0][:, t, :], tas[t], l1[:], ga_t, t)
+            fetch(bv0[:, t, :], tbs[t], l2[:], gb_t, t)
         for h in range(2):
-            product(0, h)
+            product(0, h, bv0[:, :, h * HALF:(h + 1) * HALF])
 
-        w2_d = sb.tile([P, R], U32, name="w2_d", align_bytes=64)
-        w2s_d = sb.tile([P, R], U8, name="w2s_d", align_bytes=64)
-        w_d = sb.tile([P, R], U16, name="w_d", align_bytes=64)
-        ws_d = sb.tile([P, R], U8, name="ws_d", align_bytes=64)
-        for dst, raw in ((ws_d, ws_raw), (w2_d, w2_raw), (w2s_d, w2s_raw)):
-            nc.vector.tensor_copy(out=dst[:].rearrange("p (t m) -> p t m", t=PACK),
-                                  in_=raw[:].rearrange("p (m t) -> p t m", t=PACK))
+        ws_d = deal(nc.vector.tensor_copy, ws_raw, "ws_d")
+        w2s_d = deal(nc.vector.tensor_copy, w2s_raw, "w2s_d")
+        w2_d = deal(nc.vector.tensor_copy, w2_raw, "w2_d", "m t")
 
-        parts = [(0, 0, HALF), (0, HALF, HALF), (1, 0, J), (2, 0, J), (3, 0, J)]
-        acc = [ps.tile([P, wd], F32, name="acc%d" % i) for i, (t, c0, wd) in enumerate(parts)]
+        for t in range(2, 4):
+            fetch(av[1][:, t - 2, :], tas[t], l1[:], ga_t, t)
+            for h in range(2):
+                fetch(bv1[h][:, t - 2, :], tbs[t], l2[:, h * (HALF // 16):(h + 1) * (HALF // 16)], gb_t, t)
+
+        w_d = deal(nc.scalar.copy, w_raw, "w_d", "m t")
+
+        parts = [(0, 0, HALF), (0, HALF, P), (0, HALF + P, P), (1, 0, J), (2, 0, J), (3, 0, J)]
+        acc = [ps.tile([P, wd], F32, name="acc%d" % i, tag="bank%d" % i) for i, (t, c0, wd) in enumerate(parts)]
         for i, (t, c0, wd) in enumerate(parts):
             nc.tensor.matmul_mx(out=acc[i][:], lhsT=w2_d[:, t * P:(t + 1) * P].bitcast(FP8X4),
                                 lhsT_scale=w2s_d[:, t * P:(t + 1) * P],
                                 rhs=xw[:, c0:c0 + wd].bitcast(FP4X4), rhs_scale=xs[:, c0:c0 + wd],
                                 start=True, stop=False)
 
-        for t in range(2, 4):
-            fetch(av, tas[t], l1, ga_t, t)
-            fetch(bv, tbs[t], l2, gb_t, t)
-        nc.scalar.copy(out=w_d[:].rearrange("p (t m) -> p t m", t=PACK), in_=w_raw[:].rearrange("p (m t) -> p t m", t=PACK))
         for h in range(2):
-            product(1, h)
-        for h in range(2):
-            nc.vector.quantize_mx(out=xq[:, h * HALF:(h + 1) * HALF].bitcast(FP8X4),
-                                  scales=xqs[:, h * HALF:(h + 1) * HALF],
-                                  in_=xc[h][:].rearrange("p j t -> p (j t)"))
+            product(1, h, bv1[h][:])
+        for t, c0, wd in parts[:3]:
+            nc.vector.quantize_mx(out=xq[:, c0:c0 + wd].bitcast(FP8X4), scales=xqs[:, c0:c0 + wd],
+                                  in_=xc[c0 // HALF][:, c0 % HALF:c0 % HALF + wd, :].rearrange("p j t -> p (j t)"))
 
         g1 = [sb.tile([P, J], F32, name="g1_%d" % t) for t in range(PACK)]
         for i, (t, c0, wd) in enumerate(parts):
@@ -160,31 +161,41 @@ def tile_picked_codegain_plain_bank_kept_one_posted_kernel(
                                 lhsT_scale=ws_d[:, t * P:(t + 1) * P],
                                 rhs=xq[:, c0:c0 + wd].bitcast(FP8X4), rhs_scale=xqs[:, c0:c0 + wd],
                                 start=False, stop=True)
-            if i == 0:
+            if i < 2:
                 nc.scalar.activation(out=g1[t][:, c0:c0 + wd], in_=acc[i][:], func=ACT.Relu)
             else:
                 nc.vector.tensor_scalar(out=g1[t][:, c0:c0 + wd], in0=acc[i][:], scalar1=0.0, scalar2=None, op0=ALU.max)
 
-        hv = [sb.tile([P, 2, O], BF16, name="hv%d" % u) for u in range(2)]
-        hid = sb.tile([P, O, PACK], BF16, name="hid", align_bytes=64)
-        for t in range(PACK):
-            nc.scalar.activation(out=hv[t // 2][:, t % 2, :], in_=g1[t][:].indirect(l4[:]),
-                                 func=ACT.Copy, scale=sa_t[:, t:t + 1])
-            if t % 2 == 1:
-                nc.vector.tensor_copy(out=hid[:, :, t - 1:t + 1], in_=hv[t // 2][:].rearrange("p t j -> p j t"))
+        OH = O // 2
+        hv = sb.tile([P, 3, O], BF16, name="hv")
+        hv3 = [sb.tile([P, OH], BF16, name="hv3%d" % h) for h in range(2)]
+        hid = [sb.tile([P, OH, PACK], BF16, name="hid%d" % h, align_bytes=64) for h in range(2)]
+        for t in range(3):
+            fetch(hv[:, t, :], g1[t], l4[:], sa_t, t)
+        for h in range(2):
+            nc.vector.tensor_copy(out=hid[h][:, :, 0:3], in_=hv[:, :, h * OH:(h + 1) * OH].rearrange("p t j -> p j t"))
+        for h in range(2):
+            fetch(hv3[h][:], g1[3], l4[:, h * (OH // 16):(h + 1) * (OH // 16)], sa_t, 3)
         hq = sb.tile([P, O], U32, name="hq", align_bytes=64)
         hqs = sb.tile([P, O], U8, name="hqs", align_bytes=64)
-        nc.vector.quantize_mx(out=hq[:].bitcast(FP8X4), scales=hqs[:], in_=hid[:].rearrange("p j t -> p (j t)"))
-
-        pacc = [ps.tile([P, O], F32, name="pacc%d" % t) for t in range(2)]
         pv = [sb.tile([P, O], F32, name="pv%d" % t) for t in range(2)]
+        for h in range(2):
+            nc.vector.tensor_copy(out=hid[h][:, :, 3], in_=hv3[h][:])
+        for h in range(2):
+            cols = slice(h * OH, (h + 1) * OH)
+            nc.vector.quantize_mx(out=hq[:, cols].bitcast(FP8X4), scales=hqs[:, cols], in_=hid[h][:].rearrange("p j t -> p (j t)"))
+        for h in range(2):
+            cols = slice(h * OH, (h + 1) * OH)
+            for t in range(2):
+                pacc = ps.tile([P, OH], F32, name="pacc%d%d" % (h, t), tag="pbank%d" % t if h == 0 else "bank%d" % t)
+                nc.tensor.matmul_mx(out=pacc[:], lhsT=wb_t[:, t * P:(t + 1) * P].bitcast(FP8X4),
+                                    lhsT_scale=wbs[:, t * P:(t + 1) * P],
+                                    rhs=hq[:, cols].bitcast(FP8X4), rhs_scale=hqs[:, cols], start=True, stop=True)
+                (nc.scalar.copy if h == 0 else nc.vector.tensor_copy)(out=pv[t][:, cols], in_=pacc[:])
+
         m0 = [sb.tile([P, E], F32, name="m0_%d" % t) for t in range(2)]
         for t in range(2):
-            nc.tensor.matmul_mx(out=pacc[t][:], lhsT=wb_t[:, t * P:(t + 1) * P].bitcast(FP8X4),
-                                lhsT_scale=wbs[:, t * P:(t + 1) * P],
-                                rhs=hq[:].bitcast(FP8X4), rhs_scale=hqs[:], start=True, stop=True)
-            nc.vector.tensor_copy(out=pv[t][:], in_=pacc[t][:])
-            nc.scalar.activation(out=m0[t][:], in_=pv[t][:].indirect(l5[:]), func=ACT.Copy, scale=so_t[:, t:t + 1])
+            fetch(m0[t][:], pv[t], l5[:], so_t, t)
         for t in range(2):
             nc.vector.tensor_copy(out=pages[t][:].indirect(l6[:]), in_=m0[t][:])
             nc.sync.dma_start(out=out[t * P:(t + 1) * P, :], in_=pages[t][:])

@@ -64,6 +64,10 @@ def tile_picked_codegain_plain_bank_kept_one_posted_kernel(
             copy(out=dst[:].rearrange("p (t m) -> p " + walk, t=PACK), in_=raw[:].rearrange("p (m t) -> p " + walk, t=PACK))
             return dst
 
+        warm = sb.tile([P, 2], F32, name="warm")
+        nc.vector.memset(warm[:, 0:1], 0.0)
+        nc.scalar.activation(out=warm[:, 1:2], in_=warm[:, 0:1], func=ACT.Copy)
+
         xs_win = zero_plane(M, "xs_win")
         ws_raw = zero_plane(R, "ws_raw")
         w2s_raw = zero_plane(R, "w2s_raw")

from contextlib import ExitStack

import concourse.mybir as mybir

K, J, R, T, M, O, N, E, G = 512, 512, 512, 1024, 1024, 256, 256, 128, 512
P = 128
PACK = 4
HALF = J // 2

F32 = mybir.dt.float32
BF16 = mybir.dt.bfloat16
I32 = mybir.dt.int32
U32 = mybir.dt.uint32
U16 = mybir.dt.uint16
U8 = mybir.dt.uint8
FP8X4 = mybir.dt.float8_e4m3fn_x4
FP4X4 = mybir.dt.float4_e2m1fn_x4
ACT = mybir.ActivationFunctionType
ALU = mybir.AluOpType

FLOPS = 2 * K * R * J * 2 + 2 * R * N * O


def tile_picked_codegain_plain_bank_kept_one_posted_kernel(
    tc, ta, tb, ga, gb, w_words, w_scales, xo_words, xo_scales, w2_words, w2_scales, sa,
    wb_words, wb_scales, so, offs, offs2, offs3, offs4, offs5, offs6, out,
):
    nc = tc.nc
    with ExitStack() as ctx:
        sb = ctx.enter_context(tc.tile_pool(name="sb", bufs=1))
        ps = ctx.enter_context(tc.psum_pool(name="ps", bufs=1))

        def load_list(src, name):
            t = sb.tile(list(src.shape), U16, name=name)
            nc.sync.dma_start(t[:], src)
            return t

        def load_col4(src, name, queue):
            t = sb.tile([P, PACK], F32, name=name)
            queue.dma_start(out=t[:], in_=src.rearrange("(p j) o -> p (j o)", j=PACK))
            return t

        def load_table(src, t, name):
            tl = sb.tile([P, T], F32, name=name)
            nc.sync.dma_start(out=tl[:], in_=src.rearrange("(p j) c -> p j c", j=PACK)[:, t, :])
            return tl

        def zero_plane(width, name):
            pl = sb.tile([P, width], U8, name=name, align_bytes=64)
            nc.vector.memset(pl[:].bitcast(I32), 0)
            return pl

        def load_plane(pl, src):
            for r in range(4):
                nc.sync.dma_start(out=pl[r:P:32, :].bitcast(I32), in_=src[0, r:16:4, :].bitcast(I32))

        def load_words(src, width, dtype, name):
            tl = sb.tile([P, width], dtype, name=name, align_bytes=64)
            nc.sync.dma_start(out=tl[:].bitcast(I32), in_=src.bitcast(I32))
            return tl

        def deal(copy, raw, name, walk="t m"):
            dst = sb.tile(list(raw.shape), raw.dtype, name=name, align_bytes=64)
            copy(out=dst[:].rearrange("p (t m) -> p " + walk, t=PACK), in_=raw[:].rearrange("p (m t) -> p " + walk, t=PACK))
            return dst

        warm = sb.tile([P, 2], F32, name="warm")
        nc.vector.memset(warm[:, 0:1], 0.0)
        nc.scalar.activation(out=warm[:, 1:2], in_=warm[:, 0:1], func=ACT.Copy)

        xs_win = zero_plane(M, "xs_win")
        ws_raw = zero_plane(R, "ws_raw")
        w2s_raw = zero_plane(R, "w2s_raw")
        wbs = zero_plane(N, "wbs")
        pages = [sb.tile([P, G], F32, name="page%d" % t) for t in range(2)]
        for pg in pages:
            nc.vector.memset(pg[:], 0.0)

        tas, tbs = [None] * PACK, [None] * PACK
        tas[0] = load_table(ta, 0, "ta0")
        l1 = load_list(offs, "l1")
        ga_t = load_col4(ga, "ga_t", nc.scalar)
        tbs[0] = load_table(tb, 0, "tb0")
        l2 = load_list(offs2, "l2")
        gb_t = load_col4(gb, "gb_t", nc.scalar)
        tas[1] = load_table(ta, 1, "ta1")
        xw_win = load_words(xo_words[0], M, U16, "xw_win")
        l3 = load_list(offs3, "l3")
        load_plane(xs_win, xo_scales)
        tbs[1] = load_table(tb, 1, "tb1")
        tas[2] = load_table(ta, 2, "ta2")
        load_plane(ws_raw, w_scales)
        tbs[2] = load_table(tb, 2, "tb2")
        w2_raw = load_words(w2_words[0].rearrange("p c b -> p (c b)"), R, U32, "w2_raw")
        tas[3] = load_table(ta, 3, "ta3")
        load_plane(w2s_raw, w2_scales)
        tbs[3] = load_table(tb, 3, "tb3")
        w_raw = load_words(w_words[0], R, U16, "w_raw")
        l4 = load_list(offs4, "l4")
        sa_t = load_col4(sa, "sa_t", nc.sync)
        wb_t = load_words(wb_words[0].rearrange("p c b -> p (c b)"), N, U32, "wb_t")
        load_plane(wbs, wb_scales)
        l5 = load_list(offs5, "l5")
        l6 = load_list(offs6, "l6")
        so_t = sb.tile([P, 2], F32, name="so_t")
        with nc.allow_non_contiguous_dma(reason="one value a partition for each tile of 128 rows"):
            nc.sync.dma_start(out=so_t[:], in_=so.rearrange("(t p) o -> p (t o)", p=P))

        av = [sb.tile([P, 2, J], F32, name="av%d" % u) for u in range(2)]
        bv0 = sb.tile([P, 2, J], F32, name="bv0")
        bv1 = [sb.tile([P, 2, HALF], F32, name="bv1%d" % h) for h in range(2)]
        xc = [sb.tile([P, HALF, PACK], BF16, name="xc%d" % h, align_bytes=64) for h in range(2)]
        xq = sb.tile([P, J], U32, name="xq", align_bytes=64)
        xqs = sb.tile([P, J], U8, name="xqs", align_bytes=64)

        def fetch(dst, table, offsets, scale, t):
            nc.scalar.activation(out=dst, in_=table[:].indirect(offsets), func=ACT.Copy, scale=scale[:, t:t + 1])

        def product(u, h, b_pair):
            nc.vector.tensor_tensor(
                out=xc[h][:, :, 2 * u:2 * u + 2],
                in0=av[u][:, :, h * HALF:(h + 1) * HALF].rearrange("p t j -> p j t"),
                in1=b_pair.rearrange("p t j -> p j t"),
                op=ALU.mult)

        xw = sb.tile([P, J], U16, name="xw", align_bytes=64)
        xs = sb.tile([P, J], U8, name="xs", align_bytes=64)
        nc.vector.tensor_copy(out=xw[:], in_=xw_win[:].indirect(l3[:]))
        nc.vector.tensor_copy(out=xs[:], in_=xs_win[:].indirect(l3[:]))

        for t in range(2):
            fetch(av[0][:, t, :], tas[t], l1[:], ga_t, t)
            fetch(bv0[:, t, :], tbs[t], l2[:], gb_t, t)
        for h in range(2):
            product(0, h, bv0[:, :, h * HALF:(h + 1) * HALF])

        ws_d = deal(nc.vector.tensor_copy, ws_raw, "ws_d")
        w2s_d = deal(nc.vector.tensor_copy, w2s_raw, "w2s_d")
        w2_d = deal(nc.vector.tensor_copy, w2_raw, "w2_d", "m t")

        for t in range(2, 4):
            fetch(av[1][:, t - 2, :], tas[t], l1[:], ga_t, t)
            for h in range(2):
                fetch(bv1[h][:, t - 2, :], tbs[t], l2[:, h * (HALF // 16):(h + 1) * (HALF // 16)], gb_t, t)

        w_d = deal(nc.scalar.copy, w_raw, "w_d", "m t")

        parts = [(0, 0, HALF), (0, HALF, P), (0, HALF + P, P), (1, 0, J), (2, 0, J), (3, 0, J)]
        acc = [ps.tile([P, wd], F32, name="acc%d" % i, tag="bank%d" % i) for i, (t, c0, wd) in enumerate(parts)]
        for i, (t, c0, wd) in enumerate(parts):
            nc.tensor.matmul_mx(out=acc[i][:], lhsT=w2_d[:, t * P:(t + 1) * P].bitcast(FP8X4),
                                lhsT_scale=w2s_d[:, t * P:(t + 1) * P],
                                rhs=xw[:, c0:c0 + wd].bitcast(FP4X4), rhs_scale=xs[:, c0:c0 + wd],
                                start=True, stop=False)

        for h in range(2):
            product(1, h, bv1[h][:])
        for t, c0, wd in parts[:3]:
            nc.vector.quantize_mx(out=xq[:, c0:c0 + wd].bitcast(FP8X4), scales=xqs[:, c0:c0 + wd],
                                  in_=xc[c0 // HALF][:, c0 % HALF:c0 % HALF + wd, :].rearrange("p j t -> p (j t)"))

        g1 = [sb.tile([P, J], F32, name="g1_%d" % t) for t in range(PACK)]
        for i, (t, c0, wd) in enumerate(parts):
            nc.tensor.matmul_mx(out=acc[i][:], lhsT=w_d[:, t * P:(t + 1) * P].bitcast(FP4X4),
                                lhsT_scale=ws_d[:, t * P:(t + 1) * P],
                                rhs=xq[:, c0:c0 + wd].bitcast(FP8X4), rhs_scale=xqs[:, c0:c0 + wd],
                                start=False, stop=True)
            if i < 2:
                nc.scalar.activation(out=g1[t][:, c0:c0 + wd], in_=acc[i][:], func=ACT.Relu)
            else:
                nc.vector.tensor_scalar(out=g1[t][:, c0:c0 + wd], in0=acc[i][:], scalar1=0.0, scalar2=None, op0=ALU.max)

        OH = O // 2
        hv = sb.tile([P, 3, O], BF16, name="hv")
        hv3 = [sb.tile([P, OH], BF16, name="hv3%d" % h) for h in range(2)]
        hid = [sb.tile([P, OH, PACK], BF16, name="hid%d" % h, align_bytes=64) for h in range(2)]
        for t in range(3):
            fetch(hv[:, t, :], g1[t], l4[:], sa_t, t)
        for h in range(2):
            nc.vector.tensor_copy(out=hid[h][:, :, 0:3], in_=hv[:, :, h * OH:(h + 1) * OH].rearrange("p t j -> p j t"))
        for h in range(2):
            fetch(hv3[h][:], g1[3], l4[:, h * (OH // 16):(h + 1) * (OH // 16)], sa_t, 3)
        hq = sb.tile([P, O], U32, name="hq", align_bytes=64)
        hqs = sb.tile([P, O], U8, name="hqs", align_bytes=64)
        pv = [sb.tile([P, O], F32, name="pv%d" % t) for t in range(2)]
        for h in range(2):
            nc.vector.tensor_copy(out=hid[h][:, :, 3], in_=hv3[h][:])
        for h in range(2):
            cols = slice(h * OH, (h + 1) * OH)
            nc.vector.quantize_mx(out=hq[:, cols].bitcast(FP8X4), scales=hqs[:, cols], in_=hid[h][:].rearrange("p j t -> p (j t)"))
        for h in range(2):
            cols = slice(h * OH, (h + 1) * OH)
            for t in range(2):
                pacc = ps.tile([P, OH], F32, name="pacc%d%d" % (h, t), tag="pbank%d" % t if h == 0 else "bank%d" % t)
                nc.tensor.matmul_mx(out=pacc[:], lhsT=wb_t[:, t * P:(t + 1) * P].bitcast(FP8X4),
                                    lhsT_scale=wbs[:, t * P:(t + 1) * P],
                                    rhs=hq[:, cols].bitcast(FP8X4), rhs_scale=hqs[:, cols], start=True, stop=True)
                (nc.scalar.copy if h == 0 else nc.vector.tensor_copy)(out=pv[t][:, cols], in_=pacc[:])

        m0 = [sb.tile([P, E], F32, name="m0_%d" % t) for t in range(2)]
        for t in range(2):
            fetch(m0[t][:], pv[t], l5[:], so_t, t)
        for t in range(2):
            nc.vector.tensor_copy(out=pages[t][:].indirect(l6[:]), in_=m0[t][:])
            nc.sync.dma_start(out=out[t * P:(t + 1) * P, :], in_=pages[t][:])
